import numpy as np
import ml_dtypes


def mxq(x, axis, fmt="e4m3"):
    dtype, down = {"e4m3": (ml_dtypes.float8_e4m3fn, 7), "e5m2": (ml_dtypes.float8_e5m2, 14)}[fmt]
    v = np.moveaxis(np.asarray(x, np.float32).astype(ml_dtypes.bfloat16).astype(np.float64), axis, -1)
    blocks = v.reshape(v.shape[:-1] + (-1, 32))
    amax = np.abs(blocks).max(-1, keepdims=True)
    byte = np.maximum(np.where(amax > 0, np.frexp(amax)[1] - 1 + 127, 0) - down, 1)
    scale = np.exp2(byte - 127.0)
    codes = (blocks / scale).astype(np.float32).astype(dtype).astype(np.float64)
    return np.moveaxis((codes * scale).reshape(v.shape), -1, axis)


WIDE = False


def mx_kscale(k):
    if not WIDE:
        return np.ones(k)
    levels = np.array([10, -10, 5, -5, 0])
    if k % 512:
        return np.exp2(np.random.permutation(np.resize(levels, k // 32))).repeat(32)
    a = np.empty((k // 512, 16))
    for p in range(k // 512):
        a[p, :8] = np.random.permutation(np.resize(levels, 8))
        for g in range(8):
            far = levels[np.abs(levels - a[p, g]) >= 10]
            a[p, g + 8] = far[np.random.randint(len(far))]
    return np.exp2(a.ravel()).repeat(32)


def f64(x):
    return np.asarray(x).astype(np.float64)


def striped(idx):
    return np.tile(idx.reshape(-1, 16).T, (8, 1)).astype(np.uint16)


def unstriped(offs):
    return offs[:16].T.reshape(-1).astype(np.int64)


def pack_weight(w):
    k, n = w.shape
    w = f64(np.asarray(w, np.float32).astype(ml_dtypes.bfloat16)).reshape(k // 32, 32, n)
    amax = np.abs(w).max(1)
    byte = np.clip(np.where(amax > 0, np.frexp(amax)[1] - 1 + 127 - 7, 1), 1, 254)
    scaled = (w * np.exp2(127.0 - byte)[:, None, :]).reshape(k, n).astype(np.float32)
    words = np.ascontiguousarray(scaled.reshape(k // 512, 128, 4, n).transpose(0, 1, 3, 2)).astype(ml_dtypes.float8_e4m3fn).view(np.uint8)
    return words, np.ascontiguousarray(byte.astype(np.uint8).reshape(k // 512, 16, n))


def unpack_weight(words, scales):
    g, p, n, _ = words.shape
    vals = np.ascontiguousarray(words).view(ml_dtypes.float8_e4m3fn).astype(np.float64) * np.repeat(np.exp2(scales.astype(np.float64) - 127.0), 8, axis=1)[..., None]
    return vals.transpose(0, 1, 3, 2).reshape(g * 512, n)


K, T, D, S, V, N = 512, 1024, 8, 4096, 512, 256


def setup_inputs():
    n = np.random.standard_normal
    s = mx_kscale(K)[:, None]
    words, scales = pack_weight(n((K, N)) / np.sqrt(K) / s)
    return {
        "xT": (n((K, T)) * s).astype(np.float32),
        "w_words": words,
        "w_scales": scales,
        "b": (0.3 * n((N, 1))).astype(np.float32),
        "gate": np.tile(np.random.uniform(0.2, 1.0, (D, 1, V)) / np.sqrt(D), (1, N, 1)).astype(np.float32),
        "pos1": striped(np.random.permutation(T)[:V]),
        "pos2": striped(np.random.permutation(T)[:V]),
        "pos3": striped(np.random.permutation(T)[:V]),
        "pos4": striped(np.random.permutation(T)[:V]),
        "pos5": striped(np.random.permutation(T)[:V]),
        "pos6": striped(np.random.permutation(T)[:V]),
        "pos7": striped(np.random.permutation(T)[:V]),
        "pos8": striped(np.random.permutation(T)[:V]),
    }


def reference(xT, w_words, w_scales, b, gate, pos1, pos2, pos3, pos4, pos5, pos6, pos7, pos8):
    w = unpack_weight(w_words, w_scales)
    y = w.T @ mxq(f64(xT), 0, "e4m3")
    y = y + f64(b)
    return sum(f64(gate[d]) * y[:, unstriped(p)] for d, p in enumerate((pos1, pos2, pos3, pos4, pos5, pos6, pos7, pos8)))

@@ -1,0 +1,159 @@
+from contextlib import ExitStack
+
+import concourse.mybir as mybir
+from concourse.masks import make_identity
+
+F32 = mybir.dt.float32
+BF16 = mybir.dt.bfloat16
+I32 = mybir.dt.int32
+U32 = mybir.dt.uint32
+U16 = mybir.dt.uint16
+U8 = mybir.dt.uint8
+FP8X4 = mybir.dt.float8_e4m3fn_x4
+IDENTITY = mybir.ActivationFunctionType.Identity
+MULT = mybir.AluOpType.mult
+ADD = mybir.AluOpType.add
+
+P = 128
+K, T, D, V, N = 512, 1024, 8, 512, 256
+PACK = 4
+BLOCKS = N // P
+CHUNK = 256
+PIECES = ((0, 256, 64), (256, 256, 64), (512, 256, 64), (768, 128, 48), (896, 128, 48))
+VC = V // P
+FLOPS = 2 * K * N * T + 2 * D * N * V
+
+
+def tile_picked_agg_lin_bias_sub_l_kernel(
+    tc, xT, w_words, w_scales, b, gate, pos1, pos2, pos3, pos4, pos5, pos6, pos7, pos8, out
+):
+    nc = tc.nc
+    pos = (pos1, pos2, pos3, pos4, pos5, pos6, pos7, pos8)
+
+    with ExitStack() as ctx:
+        held = ctx.enter_context(tc.tile_pool(name="held", bufs=1))
+        ring = ctx.enter_context(tc.tile_pool(name="ring", bufs=4))
+        psum = ctx.enter_context(tc.psum_pool(name="psum", bufs=8))
+
+        raws = []
+        x_view = xT.rearrange("(p j) t -> p j t", j=PACK)
+        for i in range(T // CHUNK):
+            raw = held.tile([P, PACK, CHUNK], F32, name=f"raw{i}")
+            nc.sync.dma_start(out=raw[:], in_=x_view[:, :, i * CHUNK : (i + 1) * CHUNK])
+            raws.append(raw)
+        identity = held.tile([P, P], F32, name="identity")
+        make_identity(nc, identity[:])
+        b_rows = held.tile([P, P], F32, name="b_rows")
+        nc.vector.memset(b_rows[:], 0.0)
+        w_plane = held.tile([P, N], U8, name="w_plane", align_bytes=64)
+        nc.vector.memset(w_plane[:].bitcast(I32), 0)
+        w_codes = held.tile([P, N], U32, name="w_codes", align_bytes=64)
+        nc.scalar.dma_start(out=w_codes[:].bitcast(I32), in_=w_words[0].rearrange("p m r -> p (m r)").bitcast(I32))
+        nc.scalar.dma_start(out=b_rows[0:BLOCKS, :], in_=b.rearrange("(c p) o -> c (p o)", p=P))
+        for q in range(4):
+            queue = nc.scalar if q < 2 else nc.gpsimd
+            queue.dma_start(
+                out=w_plane[32 * q : 32 * q + 4, :].bitcast(I32), in_=w_scales[0, 4 * q : 4 * q + 4, :].bitcast(I32)
+            )
+
+        lists, gates = [], [[], []]
+        for d in range(D):
+            one = held.tile([P, V // 16], U16, name=f"list{d}")
+            nc.sync.dma_start(one[:], pos[d])
+            lists.append(one)
+            g = held.tile([P, V], F32, name=f"gate0_{d}")
+            nc.sync.dma_start(out=g[:], in_=gate[d, 0:P, :])
+            gates[0].append(g)
+        for d in range(D):
+            g = held.tile([P, V], F32, name=f"gate1_{d}")
+            nc.sync.dma_start(out=g[:], in_=gate[d, P : 2 * P, :])
+            gates[1].append(g)
+
+        bias = held.tile([P, BLOCKS], F32, name="bias")
+        b_ps = psum.tile([P, P], F32, name="bank")
+        nc.tensor.transpose(b_ps[:], b_rows[:], identity[:])
+        nc.scalar.copy(bias[:], b_ps[:, 0:BLOCKS])
+
+        ys = []
+        for m in range(BLOCKS):
+            y = held.tile([P, T], F32, name=f"y{m}")
+            ys.append(y)
+        late = []
+        for i, (t0, n, on_scalar) in enumerate(PIECES):
+            grouped = held.tile([P, n, PACK], BF16, name=f"grouped{i}", align_bytes=64)
+            cut = n - on_scalar
+            first = t0 % CHUNK
+            raw = raws[t0 // CHUNK][:, :, first : first + n].rearrange("p j w -> p w j")
+            nc.scalar.copy(grouped[:, cut:n, :], raw[:, cut:n, :])
+            nc.vector.tensor_copy(grouped[:, 0:cut, :], raw[:, 0:cut, :])
+            codes = held.tile([P, n], U32, name=f"codes{i}", align_bytes=64)
+            plane = held.tile([P, n], U8, name=f"plane{i}", align_bytes=64)
+            nc.vector.quantize_mx(
+                out=codes[:].bitcast(FP8X4), scales=plane[:], in_=grouped[:].rearrange("p w j -> p (w j)")
+            )
+            for m in range(BLOCKS):
+                if m == 0:
+                    bank = psum.tile([P, n], F32, name="bank")
+                    dst = bank[:]
+                else:
+                    if i % 2 == 0:
+                        bank1 = psum.tile([P, V], F32, name="bank")
+                        width = 0
+                    dst = bank1[:, width : width + n]
+                    width += n
+                nc.tensor.matmul_mx(
+                    out=dst,
+                    lhsT=w_codes[:, m * P : (m + 1) * P].bitcast(FP8X4),
+                    lhsT_scale=w_plane[:, m * P : (m + 1) * P],
+                    rhs=codes[:].bitcast(FP8X4),
+                    rhs_scale=plane[:],
+                    start=True,
+                    stop=True,
+                )
+                if m == 0:
+                    nc.scalar.activation(ys[0][:, t0 : t0 + n], dst, IDENTITY, bias=bias[:, 0:1])
+                elif i % 2 == 1 or i == len(PIECES) - 1:
+                    late.append((bank1, t0 + n - width, width))
+        for bank1, t0, width in late:
+            nc.scalar.activation(ys[1][:, t0 : t0 + width], bank1[:, 0:width], IDENTITY, bias=bias[:, 1:2])
+
+        for m in range(BLOCKS):
+            on_pe = D if m == 0 else D - 2
+            accs = []
+            for c in range(VC):
+                acc = psum.tile([P, P], F32, name="bank")
+                accs.append(acc)
+            rest = []
+            for d in range(D):
+                prod = ring.tile([P, V], F32, name="prod")
+                nc.vector.tensor_tensor(prod[:], ys[m][:].indirect(lists[d][:]), gates[m][d][:], MULT)
+                if d < on_pe:
+                    for c in range(VC):
+                        nc.tensor.matmul(
+                            accs[c][:],
+                            prod[:, c * P : (c + 1) * P],
+                            identity[:],
+                            start=(d == 0),
+                            stop=(d == on_pe - 1),
+                            is_transpose=True,
+                        )
+                else:
+                    rest.append(prod)
+            turned = held.tile([P, V], F32, name=f"turned{m}")
+            back = psum.tile([P, V], F32, name="bank")
+            for c in range(VC):
+                nc.scalar.copy(turned[:, c * P : (c + 1) * P], accs[c][:])
+            for c in range(VC):
+                nc.tensor.transpose(back[:, c * P : (c + 1) * P], turned[:, c * P : (c + 1) * P], identity[:])
+            result = held.tile([P, V], F32, name=f"result{m}")
+            if m == 0:
+                nc.scalar.copy(result[:], back[:])
+                nc.sync.dma_start(out=out[0:P, :], in_=result[:])
+            else:
+                tail = held.tile([P, V], F32, name="tail")
+                nc.vector.tensor_tensor(tail[:], rest[0][:], rest[1][:], ADD)
+                half = V // 2
+                for h in range(2):
+                    cols = slice(h * half, (h + 1) * half)
+                    nc.vector.tensor_tensor(result[:, cols], back[:, cols], tail[:, cols], ADD)
+                    nc.sync.dma_start(out=out[P : 2 * P, cols], in_=result[:, cols])

@@ -18,8 +18,9 @@ P = 128
 K, T, D, V, N = 512, 1024, 8, 512, 256
 PACK = 4
 BLOCKS = N // P
-CHUNK = 256
-PIECES = ((0, 256, 64), (256, 256, 64), (512, 256, 64), (768, 128, 48), (896, 128, 48))
+CHUNKS = (384, 384, 256)
+STARTS = (0, 384, 768)
+GATE_RUNS = (((0, 1), (1, 2), (2, 4), (4, 8)), ((0, 4), (4, 8)))
 VC = V // P
 FLOPS = 2 * K * N * T + 2 * D * N * V
 
@@ -32,128 +33,200 @@ def tile_picked_agg_lin_bias_sub_l_kernel(
 
     with ExitStack() as ctx:
         held = ctx.enter_context(tc.tile_pool(name="held", bufs=1))
-        ring = ctx.enter_context(tc.tile_pool(name="ring", bufs=4))
         psum = ctx.enter_context(tc.psum_pool(name="psum", bufs=8))
 
-        raws = []
-        x_view = xT.rearrange("(p j) t -> p j t", j=PACK)
-        for i in range(T // CHUNK):
-            raw = held.tile([P, PACK, CHUNK], F32, name=f"raw{i}")
-            nc.sync.dma_start(out=raw[:], in_=x_view[:, :, i * CHUNK : (i + 1) * CHUNK])
-            raws.append(raw)
-        identity = held.tile([P, P], F32, name="identity")
-        make_identity(nc, identity[:])
-        b_rows = held.tile([P, P], F32, name="b_rows")
-        nc.vector.memset(b_rows[:], 0.0)
         w_plane = held.tile([P, N], U8, name="w_plane", align_bytes=64)
-        nc.vector.memset(w_plane[:].bitcast(I32), 0)
+        warm = held.tile([P, 8], F32, name="warm")
+        nc.vector.memset(warm[:], 0.0)
+        raws = []
+        for i, n in enumerate(CHUNKS):
+            raw = held.tile([P, PACK, n], F32, name=f"raw{i}")
+            raws.append(raw)
+        x_view = xT.rearrange("(p j) t -> p j t", j=PACK)
         w_codes = held.tile([P, N], U32, name="w_codes", align_bytes=64)
+        biases = []
+        for m in range(BLOCKS):
+            bias = held.tile([P, 1], F32, name=f"bias{m}")
+            biases.append(bias)
+
+        def load_x(i):
+            nc.sync.dma_start(out=raws[i][:], in_=x_view[:, :, STARTS[i] : STARTS[i] + CHUNKS[i]])
+
+        nc.scalar.dma_start(out=biases[0][:], in_=b[0:P, :])
         nc.scalar.dma_start(out=w_codes[:].bitcast(I32), in_=w_words[0].rearrange("p m r -> p (m r)").bitcast(I32))
-        nc.scalar.dma_start(out=b_rows[0:BLOCKS, :], in_=b.rearrange("(c p) o -> c (p o)", p=P))
+        load_x(0)
         for q in range(4):
-            queue = nc.scalar if q < 2 else nc.gpsimd
-            queue.dma_start(
+            nc.sync.dma_start(
                 out=w_plane[32 * q : 32 * q + 4, :].bitcast(I32), in_=w_scales[0, 4 * q : 4 * q + 4, :].bitcast(I32)
             )
+        load_x(1)
+        load_x(2)
+        warmed = held.tile([P, 8], F32, name="warmed")
+        nc.scalar.activation(warmed[:], warm[:], IDENTITY)
+        identity = held.tile([P, P], F32, name="identity")
+        make_identity(nc, identity[:])
 
-        lists, gates = [], [[], []]
+        lists = []
+        gates = []
+        for m in range(BLOCKS):
+            g = held.tile([P, D, V], F32, name=f"gates{m}")
+            gates.append(g)
         for d in range(D):
             one = held.tile([P, V // 16], U16, name=f"list{d}")
-            nc.sync.dma_start(one[:], pos[d])
             lists.append(one)
-            g = held.tile([P, V], F32, name=f"gate0_{d}")
-            nc.sync.dma_start(out=g[:], in_=gate[d, 0:P, :])
-            gates[0].append(g)
-        for d in range(D):
-            g = held.tile([P, V], F32, name=f"gate1_{d}")
-            nc.sync.dma_start(out=g[:], in_=gate[d, P : 2 * P, :])
-            gates[1].append(g)
 
-        bias = held.tile([P, BLOCKS], F32, name="bias")
-        b_ps = psum.tile([P, P], F32, name="bank")
-        nc.tensor.transpose(b_ps[:], b_rows[:], identity[:])
-        nc.scalar.copy(bias[:], b_ps[:, 0:BLOCKS])
+        def load_gates(m, d0, d1):
+            nc.sync.dma_start(
+                out=gates[m][:, d0:d1, :], in_=gate[d0:d1, m * P : (m + 1) * P, :].rearrange("d p v -> p d v")
+            )
 
-        ys = []
+        for d0, d1 in GATE_RUNS[0]:
+            for d in range(d0, d1):
+                nc.sync.dma_start(lists[d][:], pos[d])
+            load_gates(0, d0, d1)
+        nc.sync.dma_start(out=biases[1][:], in_=b[P : 2 * P, :])
+        for d0, d1 in GATE_RUNS[1]:
+            load_gates(1, d0, d1)
+
+        ys, groups, codes, planes, banks = [], [], [], [], [[], []]
         for m in range(BLOCKS):
             y = held.tile([P, T], F32, name=f"y{m}")
             ys.append(y)
-        late = []
-        for i, (t0, n, on_scalar) in enumerate(PIECES):
+        for i, n in enumerate(CHUNKS):
             grouped = held.tile([P, n, PACK], BF16, name=f"grouped{i}", align_bytes=64)
-            cut = n - on_scalar
-            first = t0 % CHUNK
-            raw = raws[t0 // CHUNK][:, :, first : first + n].rearrange("p j w -> p w j")
-            nc.scalar.copy(grouped[:, cut:n, :], raw[:, cut:n, :])
-            nc.vector.tensor_copy(grouped[:, 0:cut, :], raw[:, 0:cut, :])
-            codes = held.tile([P, n], U32, name=f"codes{i}", align_bytes=64)
+            groups.append(grouped)
+            code = held.tile([P, n], U32, name=f"codes{i}", align_bytes=64)
+            codes.append(code)
             plane = held.tile([P, n], U8, name=f"plane{i}", align_bytes=64)
-            nc.vector.quantize_mx(
-                out=codes[:].bitcast(FP8X4), scales=plane[:], in_=grouped[:].rearrange("p w j -> p (w j)")
-            )
-            for m in range(BLOCKS):
-                if m == 0:
-                    bank = psum.tile([P, n], F32, name="bank")
-                    dst = bank[:]
-                else:
-                    if i % 2 == 0:
-                        bank1 = psum.tile([P, V], F32, name="bank")
-                        width = 0
-                    dst = bank1[:, width : width + n]
-                    width += n
-                nc.tensor.matmul_mx(
-                    out=dst,
-                    lhsT=w_codes[:, m * P : (m + 1) * P].bitcast(FP8X4),
-                    lhsT_scale=w_plane[:, m * P : (m + 1) * P],
-                    rhs=codes[:].bitcast(FP8X4),
-                    rhs_scale=plane[:],
-                    start=True,
-                    stop=True,
-                )
-                if m == 0:
-                    nc.scalar.activation(ys[0][:, t0 : t0 + n], dst, IDENTITY, bias=bias[:, 0:1])
-                elif i % 2 == 1 or i == len(PIECES) - 1:
-                    late.append((bank1, t0 + n - width, width))
-        for bank1, t0, width in late:
-            nc.scalar.activation(ys[1][:, t0 : t0 + width], bank1[:, 0:width], IDENTITY, bias=bias[:, 1:2])
+            planes.append(plane)
 
+        def interleave(engine_copy, i, c0, c1):
+            engine_copy(
+                groups[i][:, c0:c1, :].rearrange("p (c i) t -> p c t i", i=4),
+                raws[i][:, :, c0:c1].rearrange("p j (c i) -> p c j i", i=4),
+            )
+
+        def quantize(i, c0, c1):
+            nc.vector.quantize_mx(
+                out=codes[i][:, c0:c1].bitcast(FP8X4),
+                scales=planes[i][:, c0:c1],
+                in_=groups[i][:, c0:c1, :].rearrange("p w j -> p (w j)"),
+            )
+
+        def multiply(m, bank, i, c0, c1, at):
+            nc.tensor.matmul_mx(
+                out=bank[:, at : at + c1 - c0],
+                lhsT=w_codes[:, m * P : (m + 1) * P].bitcast(FP8X4),
+                lhsT_scale=w_plane[:, m * P : (m + 1) * P],
+                rhs=codes[i][:, c0:c1].bitcast(FP8X4),
+                rhs_scale=planes[i][:, c0:c1],
+                start=True,
+                stop=True,
+            )
+
+        def copy_out(m, bank, t0, n):
+            nc.scalar.activation(ys[m][:, t0 : t0 + n], bank[:, 0:n], IDENTITY, bias=biases[m][:])
+
+        late = []
+
+        def project(i, pieces):
+            out_banks = []
+            for m in range(BLOCKS):
+                bank = psum.tile([P, V], F32, name="bank")
+                out_banks.append(bank)
+            for c0, c1 in pieces:
+                quantize(i, c0, c1)
+            for m in range(BLOCKS):
+                for c0, c1 in pieces:
+                    multiply(m, out_banks[m], i, c0, c1, c0)
+            late.append((out_banks[1], STARTS[i], CHUNKS[i]))
+            return out_banks[0]
+
+        interleave(nc.vector.tensor_copy, 0, 0, 384)
+        bank_0 = project(0, ((0, 256), (256, 384)))
+        interleave(nc.scalar.copy, 1, 288, 384)
+        interleave(nc.vector.tensor_copy, 1, 0, 288)
+        copy_out(0, bank_0, 0, 384)
+        bank_1 = project(1, ((0, 256), (256, 384)))
+        for c0 in (0, 128):
+            interleave(nc.scalar.copy, 2, c0 + 88, c0 + 128)
+        for c0 in (0, 128):
+            interleave(nc.vector.tensor_copy, 2, c0, c0 + 88)
+        copy_out(0, bank_1, 384, 384)
+        for c0 in (0, 128):
+            bank = psum.tile([P, P], F32, name="bank")
+            quantize(2, c0, c0 + 128)
+            multiply(0, bank, 2, c0, c0 + 128, 0)
+            copy_out(0, bank, 768 + c0, 128)
+        bank_2 = psum.tile([P, V], F32, name="bank")
+        multiply(1, bank_2, 2, 0, 256, 0)
+        late.append((bank_2, 768, 256))
+        for bank, t0, n in late:
+            copy_out(1, bank, t0, n)
+
+        half = V // 2
+        halves = (slice(0, half), slice(half, V))
+        list_halves = (slice(0, V // 32), slice(V // 32, V // 16))
         for m in range(BLOCKS):
-            on_pe = D if m == 0 else D - 2
             accs = []
             for c in range(VC):
                 acc = psum.tile([P, P], F32, name="bank")
                 accs.append(acc)
-            rest = []
-            for d in range(D):
-                prod = ring.tile([P, V], F32, name="prod")
-                nc.vector.tensor_tensor(prod[:], ys[m][:].indirect(lists[d][:]), gates[m][d][:], MULT)
-                if d < on_pe:
-                    for c in range(VC):
-                        nc.tensor.matmul(
-                            accs[c][:],
-                            prod[:, c * P : (c + 1) * P],
-                            identity[:],
-                            start=(d == 0),
-                            stop=(d == on_pe - 1),
-                            is_transpose=True,
-                        )
-                else:
-                    rest.append(prod)
-            turned = held.tile([P, V], F32, name=f"turned{m}")
-            back = psum.tile([P, V], F32, name="bank")
-            for c in range(VC):
-                nc.scalar.copy(turned[:, c * P : (c + 1) * P], accs[c][:])
-            for c in range(VC):
-                nc.tensor.transpose(back[:, c * P : (c + 1) * P], turned[:, c * P : (c + 1) * P], identity[:])
             result = held.tile([P, V], F32, name=f"result{m}")
+            turned = held.tile([P, V], F32, name=f"turned{m}")
+
+            def accumulate(prod, d, chunks, last):
+                for c in chunks:
+                    nc.tensor.matmul(
+                        accs[c][:],
+                        prod[:, c * P : (c + 1) * P],
+                        identity[:],
+                        start=(d == 0),
+                        stop=last,
+                        is_transpose=True,
+                    )
+
+            def turn_back(h):
+                back = psum.tile([P, half], F32, name="bank")
+                for c in (2 * h, 2 * h + 1):
+                    nc.scalar.copy(turned[:, c * P : (c + 1) * P], accs[c][:])
+                for c in (2 * h, 2 * h + 1):
+                    nc.tensor.transpose(
+                        back[:, (c - 2 * h) * P : (c - 2 * h + 1) * P], turned[:, c * P : (c + 1) * P], identity[:]
+                    )
+                return back
+
+            def gather(prod, m, d):
+                nc.vector.tensor_tensor(prod[:], ys[m][:].indirect(lists[d][:]), gates[m][:, d, :], MULT)
+
+            def gather_half(prod, m, d, h):
+                nc.vector.tensor_tensor(
+                    prod, ys[m][:].indirect(lists[d][:, list_halves[h]]), gates[m][:, d, halves[h]], MULT
+                )
+
             if m == 0:
-                nc.scalar.copy(result[:], back[:])
+                for d in range(D):
+                    prod = held.tile([P, V], F32, name=f"prod{m}_{d}")
+                    gather(prod, m, d)
+                    accumulate(prod, d, range(VC), d == D - 1)
+                for h in range(2):
+                    back = turn_back(h)
+                    nc.scalar.copy(result[:, halves[h]], back[:])
                 nc.sync.dma_start(out=out[0:P, :], in_=result[:])
             else:
-                tail = held.tile([P, V], F32, name="tail")
-                nc.vector.tensor_tensor(tail[:], rest[0][:], rest[1][:], ADD)
-                half = V // 2
+                for d in range(D - 2):
+                    prod = held.tile([P, V], F32, name=f"prod{m}_{d}")
+                    gather(prod, m, d)
+                    accumulate(prod, d, range(VC), False)
+                prod = held.tile([P, V], F32, name="prod1_6")
+                backs = []
                 for h in range(2):
-                    cols = slice(h * half, (h + 1) * half)
-                    nc.vector.tensor_tensor(result[:, cols], back[:, cols], tail[:, cols], ADD)
-                    nc.sync.dma_start(out=out[P : 2 * P, cols], in_=result[:, cols])
+                    gather_half(prod[:, halves[h]], m, D - 2, h)
+                    accumulate(prod, D - 2, (2 * h, 2 * h + 1), True)
+                    backs.append(turn_back(h))
+                last = held.tile([P, V], F32, name="last")
+                for h in range(2):
+                    gather_half(last[:, halves[h]], m, D - 1, h)
+                for h in range(2):
+                    nc.vector.tensor_tensor(result[:, halves[h]], backs[h][:], last[:, halves[h]], ADD)
+                    nc.sync.dma_start(out=out[P : 2 * P, halves[h]], in_=result[:, halves[h]])

from contextlib import ExitStack

import concourse.mybir as mybir
from concourse.masks import make_identity

F32 = mybir.dt.float32
BF16 = mybir.dt.bfloat16
I32 = mybir.dt.int32
U32 = mybir.dt.uint32
U16 = mybir.dt.uint16
U8 = mybir.dt.uint8
FP8X4 = mybir.dt.float8_e4m3fn_x4
IDENTITY = mybir.ActivationFunctionType.Identity
MULT = mybir.AluOpType.mult
ADD = mybir.AluOpType.add

P = 128
K, T, D, V, N = 512, 1024, 8, 512, 256
PACK = 4
BLOCKS = N // P
CHUNKS = (384, 384, 256)
STARTS = (0, 384, 768)
GATE_RUNS = (((0, 1), (1, 2), (2, 4), (4, 8)), ((0, 4), (4, 8)))
VC = V // P
FLOPS = 2 * K * N * T + 2 * D * N * V


def tile_picked_agg_lin_bias_sub_l_kernel(
    tc, xT, w_words, w_scales, b, gate, pos1, pos2, pos3, pos4, pos5, pos6, pos7, pos8, out
):
    nc = tc.nc
    pos = (pos1, pos2, pos3, pos4, pos5, pos6, pos7, pos8)

    with ExitStack() as ctx:
        held = ctx.enter_context(tc.tile_pool(name="held", bufs=1))
        psum = ctx.enter_context(tc.psum_pool(name="psum", bufs=8))

        w_plane = held.tile([P, N], U8, name="w_plane", align_bytes=64)
        warm = held.tile([P, 8], F32, name="warm")
        nc.vector.memset(warm[:], 0.0)
        raws = []
        for i, n in enumerate(CHUNKS):
            raw = held.tile([P, PACK, n], F32, name=f"raw{i}")
            raws.append(raw)
        x_view = xT.rearrange("(p j) t -> p j t", j=PACK)
        w_codes = held.tile([P, N], U32, name="w_codes", align_bytes=64)
        biases = []
        for m in range(BLOCKS):
            bias = held.tile([P, 1], F32, name=f"bias{m}")
            biases.append(bias)

        def load_x(i):
            nc.sync.dma_start(out=raws[i][:], in_=x_view[:, :, STARTS[i] : STARTS[i] + CHUNKS[i]])

        nc.scalar.dma_start(out=biases[0][:], in_=b[0:P, :])
        nc.scalar.dma_start(out=w_codes[:].bitcast(I32), in_=w_words[0].rearrange("p m r -> p (m r)").bitcast(I32))
        load_x(0)
        for q in range(4):
            nc.sync.dma_start(
                out=w_plane[32 * q : 32 * q + 4, :].bitcast(I32), in_=w_scales[0, 4 * q : 4 * q + 4, :].bitcast(I32)
            )
        load_x(1)
        load_x(2)
        warmed = held.tile([P, 8], F32, name="warmed")
        nc.scalar.activation(warmed[:], warm[:], IDENTITY)
        identity = held.tile([P, P], F32, name="identity")
        make_identity(nc, identity[:])

        lists = []
        gates = []
        for m in range(BLOCKS):
            g = held.tile([P, D, V], F32, name=f"gates{m}")
            gates.append(g)
        for d in range(D):
            one = held.tile([P, V // 16], U16, name=f"list{d}")
            lists.append(one)

        def load_gates(m, d0, d1):
            nc.sync.dma_start(
                out=gates[m][:, d0:d1, :], in_=gate[d0:d1, m * P : (m + 1) * P, :].rearrange("d p v -> p d v")
            )

        for d0, d1 in GATE_RUNS[0]:
            for d in range(d0, d1):
                nc.sync.dma_start(lists[d][:], pos[d])
            load_gates(0, d0, d1)
        nc.sync.dma_start(out=biases[1][:], in_=b[P : 2 * P, :])
        for d0, d1 in GATE_RUNS[1]:
            load_gates(1, d0, d1)

        ys, groups, codes, planes, banks = [], [], [], [], [[], []]
        for m in range(BLOCKS):
            y = held.tile([P, T], F32, name=f"y{m}")
            ys.append(y)
        for i, n in enumerate(CHUNKS):
            grouped = held.tile([P, n, PACK], BF16, name=f"grouped{i}", align_bytes=64)
            groups.append(grouped)
            code = held.tile([P, n], U32, name=f"codes{i}", align_bytes=64)
            codes.append(code)
            plane = held.tile([P, n], U8, name=f"plane{i}", align_bytes=64)
            planes.append(plane)

        def interleave(engine_copy, i, c0, c1):
            engine_copy(
                groups[i][:, c0:c1, :].rearrange("p (c i) t -> p c t i", i=4),
                raws[i][:, :, c0:c1].rearrange("p j (c i) -> p c j i", i=4),
            )

        def quantize(i, c0, c1):
            nc.vector.quantize_mx(
                out=codes[i][:, c0:c1].bitcast(FP8X4),
                scales=planes[i][:, c0:c1],
                in_=groups[i][:, c0:c1, :].rearrange("p w j -> p (w j)"),
            )

        def multiply(m, bank, i, c0, c1, at):
            nc.tensor.matmul_mx(
                out=bank[:, at : at + c1 - c0],
                lhsT=w_codes[:, m * P : (m + 1) * P].bitcast(FP8X4),
                lhsT_scale=w_plane[:, m * P : (m + 1) * P],
                rhs=codes[i][:, c0:c1].bitcast(FP8X4),
                rhs_scale=planes[i][:, c0:c1],
                start=True,
                stop=True,
            )

        def copy_out(m, bank, t0, n):
            nc.scalar.activation(ys[m][:, t0 : t0 + n], bank[:, 0:n], IDENTITY, bias=biases[m][:])

        late = []

        def project(i, pieces):
            out_banks = []
            for m in range(BLOCKS):
                bank = psum.tile([P, V], F32, name="bank")
                out_banks.append(bank)
            for c0, c1 in pieces:
                quantize(i, c0, c1)
            for m in range(BLOCKS):
                for c0, c1 in pieces:
                    multiply(m, out_banks[m], i, c0, c1, c0)
            late.append((out_banks[1], STARTS[i], CHUNKS[i]))
            return out_banks[0]

        interleave(nc.vector.tensor_copy, 0, 0, 384)
        bank_0 = project(0, ((0, 256), (256, 384)))
        interleave(nc.scalar.copy, 1, 288, 384)
        interleave(nc.vector.tensor_copy, 1, 0, 288)
        copy_out(0, bank_0, 0, 384)
        bank_1 = project(1, ((0, 256), (256, 384)))
        for c0 in (0, 128):
            interleave(nc.scalar.copy, 2, c0 + 88, c0 + 128)
        for c0 in (0, 128):
            interleave(nc.vector.tensor_copy, 2, c0, c0 + 88)
        copy_out(0, bank_1, 384, 384)
        for c0 in (0, 128):
            bank = psum.tile([P, P], F32, name="bank")
            quantize(2, c0, c0 + 128)
            multiply(0, bank, 2, c0, c0 + 128, 0)
            copy_out(0, bank, 768 + c0, 128)
        bank_2 = psum.tile([P, V], F32, name="bank")
        multiply(1, bank_2, 2, 0, 256, 0)
        late.append((bank_2, 768, 256))
        for bank, t0, n in late:
            copy_out(1, bank, t0, n)

        half = V // 2
        halves = (slice(0, half), slice(half, V))
        list_halves = (slice(0, V // 32), slice(V // 32, V // 16))
        for m in range(BLOCKS):
            accs = []
            for c in range(VC):
                acc = psum.tile([P, P], F32, name="bank")
                accs.append(acc)
            result = held.tile([P, V], F32, name=f"result{m}")
            turned = held.tile([P, V], F32, name=f"turned{m}")

            def accumulate(prod, d, chunks, last):
                for c in chunks:
                    nc.tensor.matmul(
                        accs[c][:],
                        prod[:, c * P : (c + 1) * P],
                        identity[:],
                        start=(d == 0),
                        stop=last,
                        is_transpose=True,
                    )

            def turn_back(h):
                back = psum.tile([P, half], F32, name="bank")
                for c in (2 * h, 2 * h + 1):
                    nc.scalar.copy(turned[:, c * P : (c + 1) * P], accs[c][:])
                for c in (2 * h, 2 * h + 1):
                    nc.tensor.transpose(
                        back[:, (c - 2 * h) * P : (c - 2 * h + 1) * P], turned[:, c * P : (c + 1) * P], identity[:]
                    )
                return back

            def gather(prod, m, d):
                nc.vector.tensor_tensor(prod[:], ys[m][:].indirect(lists[d][:]), gates[m][:, d, :], MULT)

            def gather_half(prod, m, d, h):
                nc.vector.tensor_tensor(
                    prod, ys[m][:].indirect(lists[d][:, list_halves[h]]), gates[m][:, d, halves[h]], MULT
                )

            if m == 0:
                for d in range(D):
                    prod = held.tile([P, V], F32, name=f"prod{m}_{d}")
                    gather(prod, m, d)
                    accumulate(prod, d, range(VC), d == D - 1)
                for h in range(2):
                    back = turn_back(h)
                    nc.scalar.copy(result[:, halves[h]], back[:])
                nc.sync.dma_start(out=out[0:P, :], in_=result[:])
            else:
                for d in range(D - 2):
                    prod = held.tile([P, V], F32, name=f"prod{m}_{d}")
                    gather(prod, m, d)
                    accumulate(prod, d, range(VC), False)
                prod = held.tile([P, V], F32, name="prod1_6")
                backs = []
                for h in range(2):
                    gather_half(prod[:, halves[h]], m, D - 2, h)
                    accumulate(prod, D - 2, (2 * h, 2 * h + 1), True)
                    backs.append(turn_back(h))
                last = held.tile([P, V], F32, name="last")
                for h in range(2):
                    gather_half(last[:, halves[h]], m, D - 1, h)
                for h in range(2):
                    nc.vector.tensor_tensor(result[:, halves[h]], backs[h][:], last[:, halves[h]], ADD)
                    nc.sync.dma_start(out=out[P : 2 * P, halves[h]], in_=result[:, halves[h]])
